import numpy as np
import ml_dtypes


def mxq(x, axis, fmt="e4m3"):
    dtype, down = {"e4m3": (ml_dtypes.float8_e4m3fn, 7), "e5m2": (ml_dtypes.float8_e5m2, 14)}[fmt]
    v = np.moveaxis(np.asarray(x, np.float32).astype(ml_dtypes.bfloat16).astype(np.float64), axis, -1)
    blocks = v.reshape(v.shape[:-1] + (-1, 32))
    amax = np.abs(blocks).max(-1, keepdims=True)
    byte = np.maximum(np.where(amax > 0, np.frexp(amax)[1] - 1 + 127, 0) - down, 1)
    scale = np.exp2(byte - 127.0)
    codes = (blocks / scale).astype(np.float32).astype(dtype).astype(np.float64)
    return np.moveaxis((codes * scale).reshape(v.shape), -1, axis)


WIDE = False


def mx_kscale(k):
    if not WIDE:
        return np.ones(k)
    levels = np.array([10, -10, 5, -5, 0])
    if k % 512:
        return np.exp2(np.random.permutation(np.resize(levels, k // 32))).repeat(32)
    a = np.empty((k // 512, 16))
    for p in range(k // 512):
        a[p, :8] = np.random.permutation(np.resize(levels, 8))
        for g in range(8):
            far = levels[np.abs(levels - a[p, g]) >= 10]
            a[p, g + 8] = far[np.random.randint(len(far))]
    return np.exp2(a.ravel()).repeat(32)


def f64(x):
    return np.asarray(x).astype(np.float64)


def striped(idx):
    return np.tile(np.asarray(idx).reshape(-1, 16).T, (8, 1)).astype(np.uint16)


def unstriped(offs):
    return offs[:16].T.reshape(-1).astype(np.int64)


E2M1 = np.array([0.0, 0.5, 1.0, 1.5, 2.0, 3.0, 4.0, 6.0, -0.0, -0.5, -1.0, -1.5, -2.0, -3.0, -4.0, -6.0])


def pack_weight(w, fmt):
    k, n = w.shape
    w = f64(np.asarray(w, np.float32).astype(ml_dtypes.bfloat16)).reshape(k // 32, 32, n)
    amax = np.abs(w).max(1)
    if fmt == "e4m3":
        byte = np.frexp(amax)[1] - 1 + 127 - 7
    else:
        mant, ex = np.frexp(amax / 6.0)
        byte = np.where(mant > 0.5, ex, ex - 1) + 127
    byte = np.clip(np.where(amax > 0, byte, 1), 1, 254)
    scaled = (w * np.exp2(127.0 - byte)[:, None, :]).reshape(k, n).astype(np.float32)
    by_word = np.ascontiguousarray(scaled.reshape(k // 512, 128, 4, n).transpose(0, 1, 3, 2))
    if fmt == "e4m3":
        words = by_word.astype(ml_dtypes.float8_e4m3fn).view(np.uint8)
    else:
        c = by_word.astype(ml_dtypes.float4_e2m1fn).view(np.uint8) & 0xF
        words = (c[..., 0::2] | (c[..., 1::2] << 4)).reshape(k // 512, 128, 2 * n)
    return np.ascontiguousarray(words), np.ascontiguousarray(byte.astype(np.uint8).reshape(k // 512, 16, n))


def unpack_weight(words, scales, fmt):
    g, _, n = scales.shape
    words = np.ascontiguousarray(words).reshape(g, 128, n, -1)
    if fmt == "e4m3":
        vals = words.view(ml_dtypes.float8_e4m3fn).astype(np.float64)
    else:
        nib = np.empty((g, 128, n, 4), np.uint8)
        nib[..., 0::2] = words & 0xF
        nib[..., 1::2] = words >> 4
        vals = E2M1[nib]
    vals = vals * np.repeat(np.exp2(scales.astype(np.float64) - 127.0), 8, axis=1)[..., None]
    return vals.transpose(0, 1, 3, 2).reshape(g * 512, n)


def softplus(v):
    return np.log(1.0 + np.exp(v))


B, N, T, D, NQ = 1, 512, 2048, 1024, 128


def setup_inputs():
    n = np.random.standard_normal
    idx = np.random.permutation(T)[:B * N]
    idx2 = np.random.permutation(1024)[:B * N]
    s = mx_kscale(D)[:, None]
    kp = pack_weight(n((D, T)) / s, "e2m1")
    cp = pack_weight(n((D, 1024)) / s, "e2m1")
    return {
        "qT": (n((B, D, NQ)) * s * (1.00 / np.sqrt(D))).astype(np.float32),
        "k_words": np.ascontiguousarray(kp[0].reshape(1, 2, 128, T, 2).transpose(0, 2, 3, 1, 4)).reshape(1, 128, T, 4),
        "k_scales": kp[1],
        "c_words": np.ascontiguousarray(cp[0].reshape(1, 2, 128, 1024, 2).transpose(0, 2, 3, 1, 4)).reshape(1, 128, 1024, 4),
        "c_scales": cp[1],
        "rw": (np.random.uniform(0.2, 2.0, (B, NQ, 1))).astype(np.float32),
        "offs": striped(idx),
        "offs2": striped(idx2),
    }


def reference(qT, k_words, k_scales, c_words, c_scales, rw, offs, offs2):
    idx = unstriped(offs)
    idx2 = unstriped(offs2)
    pick = lambda x, which: x[:, which].reshape(x.shape[0], B, -1).transpose(1, 0, 2)
    k = unpack_weight(k_words.reshape(1, 128, T, 2, 2).transpose(0, 3, 1, 2, 4).reshape(2, 128, 2 * T), k_scales, "e2m1")
    kg = pick(k, idx)
    c = unpack_weight(c_words.reshape(1, 128, 1024, 2, 2).transpose(0, 3, 1, 2, 4).reshape(2, 128, 2 * 1024), c_scales, "e2m1")
    cg = pick(c, idx2)
    qq = mxq(f64(qT), 1, "e4m3")
    a = qq.transpose(0, 2, 1) @ kg
    z = qq.transpose(0, 2, 1) @ cg
    y = softplus(z - a) * f64(rw)
    return y

@@ -1,0 +1,136 @@
+import math
+
+import concourse.mybir as mybir
+
+F32 = mybir.dt.float32
+BF16 = mybir.dt.bfloat16
+I32 = mybir.dt.int32
+U32 = mybir.dt.uint32
+U16 = mybir.dt.uint16
+U8 = mybir.dt.uint8
+FP8X4 = mybir.dt.float8_e4m3fn_x4
+FP4X4 = mybir.dt.float4_e2m1fn_x4
+ACT = mybir.ActivationFunctionType
+ALU = mybir.AluOpType
+
+P = 128
+NQ = 128
+SLOTS = 512
+PASSES = 2
+PACK = 4
+SHIFT = 16
+CAP = 40.0
+GROUP = 128
+GROUPS = SLOTS // GROUP
+
+FLOPS = 2 * 2 * NQ * SLOTS * 1024
+
+
+def tile_attend_logrank_topk_kernel(tc, qT, k_words, k_scales, c_words, c_scales, rw, offs, offs2, out):
+    nc = tc.nc
+    with (
+        tc.tile_pool(name="sbuf", bufs=1) as sbuf,
+        tc.psum_pool(name="psum", bufs=1) as psum,
+    ):
+        def load_list(src, name):
+            t = sbuf.tile([P, SLOTS // 16], U16, name=name)
+            nc.sync.dma_start(t[:], src)
+            return t
+
+        def load_scales(src, queues, name):
+            items = src.shape[2]
+            t = sbuf.tile([P, items], U8, name=name, align_bytes=64)
+            nc.vector.memset(t[:].bitcast(I32), 0)
+            rows = src.rearrange("o (q r) t -> r q o t", r=4)
+            for r in range(4):
+                queues[r].dma_start(t[r:P:SHIFT, :].bitcast(I32), rows[r].bitcast(I32))
+            return t
+
+        def load_words(src, queue, name):
+            t = sbuf.tile([P, src.shape[2]], U32, name=name, align_bytes=64)
+            queue.dma_start(t[:].bitcast(I32), src[0].rearrange("p t b -> p (t b)").bitcast(I32))
+            return t
+
+        def gather_scales(window, idx, runs, name):
+            first = sbuf.tile([P, SLOTS], U8, name=name + "_pass0", align_bytes=64)
+            second = sbuf.tile([P, SLOTS], U8, name=name + "_pass1", align_bytes=64)
+            nc.vector.memset(second[:].bitcast(I32), 0)
+            nc.vector.tensor_copy(first[:], window[:].indirect(idx[:]))
+            for lo, hi in runs:
+                nc.sync.dma_start(second[lo:hi, :].bitcast(I32), first[lo + SHIFT : hi + SHIFT, :].bitcast(I32))
+            return [first, second]
+
+        def gather_words(window, idx, first, count, name):
+            pairs = sbuf.tile([P, count], U32, name=name + "_pairs", align_bytes=64)
+            nc.vector.tensor_copy(pairs[:], window[:].indirect(idx[:, first // 16 : (first + count) // 16]))
+            words = sbuf.tile([P, PASSES, count], U16, name=name + "_words", align_bytes=64)
+            nc.vector.tensor_copy(words[:], pairs[:].bitcast(U16).rearrange("p (n o) -> p o n", o=PASSES))
+            return [words[:, :, g : g + GROUP] for g in range(0, count, GROUP)]
+
+        def quantise(raw, sign, name):
+            rounded = sbuf.tile([P, PASSES, NQ, PACK], BF16, name=name + "_bf16", align_bytes=64)
+            nc.scalar.activation(rounded[:], raw[:].rearrange("p o j q -> p o q j"), ACT.Copy, scale=sign)
+            codes = sbuf.tile([P, PASSES * NQ], U32, name=name + "_codes", align_bytes=64)
+            scales = sbuf.tile([P, PASSES * NQ], U8, name=name + "_scales", align_bytes=64)
+            nc.vector.quantize_mx(
+                out=codes[:].bitcast(FP8X4), scales=scales[:], in_=rounded[:].rearrange("p o q j -> p (o q j)")
+            )
+            return codes, scales
+
+        c_list = load_list(offs2, "c_list")
+        k_list = load_list(offs, "k_list")
+        c_scale_window = load_scales(c_scales, [nc.sync, nc.sync, nc.sync, nc.sync], "c_scale_window")
+        c_word_window = load_words(c_words, nc.sync, "c_word_window")
+        q_raw = sbuf.tile([P, PASSES, PACK, NQ], F32, name="q_raw")
+        nc.sync.dma_start(q_raw[:], qT[0].rearrange("(o p j) q -> p o j q", o=PASSES, j=PACK))
+        k_scale_window = load_scales(k_scales, [nc.sync, nc.sync, nc.sync, nc.sync], "k_scale_window")
+        k_word_window = load_words(k_words, nc.sync, "k_word_window")
+        weight = sbuf.tile([P, 1], F32, name="weight")
+        nc.sync.dma_start(weight[:], rw[0])
+
+        diffs = [psum.tile([NQ, GROUP], F32, name=f"diff{g}") for g in range(GROUPS)]
+
+        def multiply(g, query, words, planes, opens):
+            codes, scales = query
+            for o in range(PASSES):
+                cols = slice(o * NQ, (o + 1) * NQ)
+                nc.tensor.matmul_mx(
+                    out=diffs[g][:],
+                    lhsT=codes[:, cols].bitcast(FP8X4),
+                    lhsT_scale=scales[:, cols],
+                    rhs=words[:, o, :].bitcast(FP4X4),
+                    rhs_scale=planes[o][:, g * GROUP : (g + 1) * GROUP],
+                    start=(opens and o == 0),
+                    stop=(not opens and o == PASSES - 1),
+                )
+
+        half = SLOTS // 2
+        c_planes = gather_scales(c_scale_window, c_list, [(0, 112)], "c_scale")
+        c_listed = gather_words(c_word_window, c_list, 0, SLOTS, "c")
+        k_planes = gather_scales(k_scale_window, k_list, [(0, 64), (64, 68), (96, 100)], "k_scale")
+        q_plus = quantise(q_raw, 1.0, "q_plus")
+        q_minus = quantise(q_raw, -1.0, "q_minus")
+        for g in range(GROUPS):
+            multiply(g, q_plus, c_listed[g], c_planes, True)
+        k_listed = []
+        for h in range(2):
+            k_listed.extend(gather_words(k_word_window, k_list, h * half, half, f"k{h}"))
+
+        grown = sbuf.tile([NQ, SLOTS], F32, name="grown")
+        beyond = sbuf.tile([NQ, SLOTS], F32, name="beyond")
+        for g in range(GROUPS):
+            multiply(g, q_minus, k_listed[g], k_planes, False)
+            nc.scalar.activation(grown[:, g * GROUP : (g + 1) * GROUP], diffs[g][:], ACT.Exp)
+        capped = sbuf.tile([NQ, SLOTS], F32, name="capped")
+        nc.vector.tensor_scalar(capped[:], grown[:], math.exp(CAP), 1.0, ALU.min, ALU.add)
+        for g in range(GROUPS):
+            nc.vector.tensor_scalar(beyond[:, g * GROUP : (g + 1) * GROUP], diffs[g][:], CAP, -CAP, ALU.max, ALU.add)
+        beyond_w = sbuf.tile([NQ, SLOTS], F32, name="beyond_w")
+        nc.vector.tensor_scalar(beyond_w[:], beyond[:], weight[:], None, ALU.mult)
+        for h in range(2):
+            cols = slice(h * half, (h + 1) * half)
+            logs = sbuf.tile([NQ, half], F32, name=f"logs{h}")
+            nc.scalar.activation(logs[:], capped[:, cols], ACT.Ln)
+            result = sbuf.tile([NQ, half], F32, name=f"result{h}")
+            nc.vector.scalar_tensor_tensor(result[:], logs[:], weight[:], beyond_w[:, cols], ALU.mult, ALU.add)
+            nc.sync.dma_start(out[0][:, cols], result[:])

@@ -37,13 +37,10 @@ def tile_attend_logrank_topk_kernel(tc, qT, k_words, k_scales, c_words, c_scales
             nc.sync.dma_start(t[:], src)
             return t
 
-        def load_scales(src, queues, name):
-            items = src.shape[2]
-            t = sbuf.tile([P, items], U8, name=name, align_bytes=64)
-            nc.vector.memset(t[:].bitcast(I32), 0)
-            rows = src.rearrange("o (q r) t -> r q o t", r=4)
-            for r in range(4):
-                queues[r].dma_start(t[r:P:SHIFT, :].bitcast(I32), rows[r].bitcast(I32))
+        def load_scales(src, zeroing, name):
+            t = sbuf.tile([P, src.shape[2]], U8, name=name, align_bytes=64)
+            zeroing.memset(t[:].bitcast(I32), 0)
+            nc.sync.dma_start(t[0:P:4, :].bitcast(I32), src.rearrange("o f t -> f o t").bitcast(I32))
             return t
 
         def load_words(src, queue, name):
@@ -51,24 +48,27 @@ def tile_attend_logrank_topk_kernel(tc, qT, k_words, k_scales, c_words, c_scales
             queue.dma_start(t[:].bitcast(I32), src[0].rearrange("p t b -> p (t b)").bitcast(I32))
             return t
 
-        def gather_scales(window, idx, runs, name):
-            first = sbuf.tile([P, SLOTS], U8, name=name + "_pass0", align_bytes=64)
-            second = sbuf.tile([P, SLOTS], U8, name=name + "_pass1", align_bytes=64)
-            nc.vector.memset(second[:].bitcast(I32), 0)
-            nc.vector.tensor_copy(first[:], window[:].indirect(idx[:]))
-            for lo, hi in runs:
-                nc.sync.dma_start(second[lo:hi, :].bitcast(I32), first[lo + SHIFT : hi + SHIFT, :].bitcast(I32))
-            return [first, second]
+        def gather_scales(window, idx, queues, name):
+            listed = sbuf.tile([P, SLOTS], U8, name=name + "_listed", align_bytes=64)
+            planes = sbuf.tile([P, PASSES, SLOTS], U8, name=name + "_planes", align_bytes=64)
+            nc.vector.memset(planes[:].rearrange("p o n -> p (o n)").bitcast(I32), 0)
+            nc.vector.tensor_copy(listed[:], window[:].indirect(idx[:]))
+            for quadrant in range(4):
+                first = 32 * quadrant
+                queues[quadrant].dma_start(
+                    planes[first : first + 4, :, :].bitcast(I32), listed[first : first + 32 : 4, :].bitcast(I32)
+                )
+            return planes
 
-        def gather_words(window, idx, first, count, name):
-            pairs = sbuf.tile([P, count], U32, name=name + "_pairs", align_bytes=64)
+        def gather_words(window, idx, first, count, name, tag):
+            pairs = sbuf.tile([P, count], U32, name=name + "_pairs", tag=tag, align_bytes=64)
             nc.vector.tensor_copy(pairs[:], window[:].indirect(idx[:, first // 16 : (first + count) // 16]))
             words = sbuf.tile([P, PASSES, count], U16, name=name + "_words", align_bytes=64)
             nc.vector.tensor_copy(words[:], pairs[:].bitcast(U16).rearrange("p (n o) -> p o n", o=PASSES))
             return [words[:, :, g : g + GROUP] for g in range(0, count, GROUP)]
 
         def quantise(raw, sign, name):
-            rounded = sbuf.tile([P, PASSES, NQ, PACK], BF16, name=name + "_bf16", align_bytes=64)
+            rounded = sbuf.tile([P, PASSES, NQ, PACK], BF16, name=name + "_bf16", tag=name + "_bf16", align_bytes=64)
             nc.scalar.activation(rounded[:], raw[:].rearrange("p o j q -> p o q j"), ACT.Copy, scale=sign)
             codes = sbuf.tile([P, PASSES * NQ], U32, name=name + "_codes", align_bytes=64)
             scales = sbuf.tile([P, PASSES * NQ], U8, name=name + "_scales", align_bytes=64)
@@ -79,14 +79,14 @@ def tile_attend_logrank_topk_kernel(tc, qT, k_words, k_scales, c_words, c_scales
 
         c_list = load_list(offs2, "c_list")
         k_list = load_list(offs, "k_list")
-        c_scale_window = load_scales(c_scales, [nc.sync, nc.sync, nc.sync, nc.sync], "c_scale_window")
+        weight = sbuf.tile([P, 1], F32, name="weight")
+        nc.sync.dma_start(weight[:], rw[0])
+        c_scale_window = load_scales(c_scales, nc.vector, "c_scale_window")
+        k_scale_window = load_scales(k_scales, nc.gpsimd, "k_scale_window")
         c_word_window = load_words(c_words, nc.sync, "c_word_window")
         q_raw = sbuf.tile([P, PASSES, PACK, NQ], F32, name="q_raw")
         nc.sync.dma_start(q_raw[:], qT[0].rearrange("(o p j) q -> p o j q", o=PASSES, j=PACK))
-        k_scale_window = load_scales(k_scales, [nc.sync, nc.sync, nc.sync, nc.sync], "k_scale_window")
         k_word_window = load_words(k_words, nc.sync, "k_word_window")
-        weight = sbuf.tile([P, 1], F32, name="weight")
-        nc.sync.dma_start(weight[:], rw[0])
 
         diffs = [psum.tile([NQ, GROUP], F32, name=f"diff{g}") for g in range(GROUPS)]
 
@@ -99,22 +99,22 @@ def tile_attend_logrank_topk_kernel(tc, qT, k_words, k_scales, c_words, c_scales
                     lhsT=codes[:, cols].bitcast(FP8X4),
                     lhsT_scale=scales[:, cols],
                     rhs=words[:, o, :].bitcast(FP4X4),
-                    rhs_scale=planes[o][:, g * GROUP : (g + 1) * GROUP],
+                    rhs_scale=planes[:, o, g * GROUP : (g + 1) * GROUP],
                     start=(opens and o == 0),
                     stop=(not opens and o == PASSES - 1),
                 )
 
         half = SLOTS // 2
-        c_planes = gather_scales(c_scale_window, c_list, [(0, 112)], "c_scale")
-        c_listed = gather_words(c_word_window, c_list, 0, SLOTS, "c")
-        k_planes = gather_scales(k_scale_window, k_list, [(0, 64), (64, 68), (96, 100)], "k_scale")
+        c_planes = gather_scales(c_scale_window, c_list, [nc.sync] * 4, "c_scale")
+        k_planes = gather_scales(k_scale_window, k_list, [nc.sync] * 4, "k_scale")
+        c_listed = gather_words(c_word_window, c_list, 0, SLOTS, "c", "c_pairs")
         q_plus = quantise(q_raw, 1.0, "q_plus")
         q_minus = quantise(q_raw, -1.0, "q_minus")
         for g in range(GROUPS):
             multiply(g, q_plus, c_listed[g], c_planes, True)
         k_listed = []
         for h in range(2):
-            k_listed.extend(gather_words(k_word_window, k_list, h * half, half, f"k{h}"))
+            k_listed.extend(gather_words(k_word_window, k_list, h * half, half, f"k{h}", ["q_plus_bf16", "q_minus_bf16"][h]))
 
         grown = sbuf.tile([NQ, SLOTS], F32, name="grown")
         beyond = sbuf.tile([NQ, SLOTS], F32, name="beyond")
@@ -127,10 +127,10 @@ def tile_attend_logrank_topk_kernel(tc, qT, k_words, k_scales, c_words, c_scales
             nc.vector.tensor_scalar(beyond[:, g * GROUP : (g + 1) * GROUP], diffs[g][:], CAP, -CAP, ALU.max, ALU.add)
         beyond_w = sbuf.tile([NQ, SLOTS], F32, name="beyond_w")
         nc.vector.tensor_scalar(beyond_w[:], beyond[:], weight[:], None, ALU.mult)
-        for h in range(2):
-            cols = slice(h * half, (h + 1) * half)
-            logs = sbuf.tile([NQ, half], F32, name=f"logs{h}")
+        for g in range(GROUPS):
+            cols = slice(g * GROUP, (g + 1) * GROUP)
+            logs = sbuf.tile([NQ, GROUP], F32, name=f"logs{g}")
             nc.scalar.activation(logs[:], capped[:, cols], ACT.Ln)
-            result = sbuf.tile([NQ, half], F32, name=f"result{h}")
+            result = sbuf.tile([NQ, GROUP], F32, name=f"result{g}")
             nc.vector.scalar_tensor_tensor(result[:], logs[:], weight[:], beyond_w[:, cols], ALU.mult, ALU.add)
             nc.sync.dma_start(out[0][:, cols], result[:])

@@ -37,9 +37,9 @@ def tile_attend_logrank_topk_kernel(tc, qT, k_words, k_scales, c_words, c_scales
             nc.sync.dma_start(t[:], src)
             return t
 
-        def load_scales(src, zeroing, name):
-            t = sbuf.tile([P, src.shape[2]], U8, name=name, align_bytes=64)
-            zeroing.memset(t[:].bitcast(I32), 0)
+        def load_scales(src, name):
+            t = sbuf.tile([P, src.shape[2]], U8, name=name, tag=name, align_bytes=64)
+            nc.vector.memset(t[:].bitcast(I32), 0)
             nc.sync.dma_start(t[0:P:4, :].bitcast(I32), src.rearrange("o f t -> f o t").bitcast(I32))
             return t
 
@@ -60,40 +60,39 @@ def tile_attend_logrank_topk_kernel(tc, qT, k_words, k_scales, c_words, c_scales
                 )
             return planes
 
-        def gather_words(window, idx, first, count, name, tag):
-            pairs = sbuf.tile([P, count], U32, name=name + "_pairs", tag=tag, align_bytes=64)
-            nc.vector.tensor_copy(pairs[:], window[:].indirect(idx[:, first // 16 : (first + count) // 16]))
-            words = sbuf.tile([P, PASSES, count], U16, name=name + "_words", align_bytes=64)
-            nc.vector.tensor_copy(words[:], pairs[:].bitcast(U16).rearrange("p (n o) -> p o n", o=PASSES))
-            return [words[:, :, g : g + GROUP] for g in range(0, count, GROUP)]
+        def gather_words(window, idx, gathers, name, tag):
+            pairs = sbuf.tile([P, SLOTS], U32, name=name + "_pairs", tag=tag, align_bytes=64)
+            columns = SLOTS // 16 // gathers
+            for n in range(gathers):
+                part = idx[:, n * columns : (n + 1) * columns]
+                nc.vector.tensor_copy(pairs[:, 16 * n * columns : 16 * (n + 1) * columns], window[:].indirect(part))
+            return pairs
 
-        def quantise(raw, sign, name):
-            rounded = sbuf.tile([P, PASSES, NQ, PACK], BF16, name=name + "_bf16", tag=name + "_bf16", align_bytes=64)
-            nc.scalar.activation(rounded[:], raw[:].rearrange("p o j q -> p o q j"), ACT.Copy, scale=sign)
-            codes = sbuf.tile([P, PASSES * NQ], U32, name=name + "_codes", align_bytes=64)
-            scales = sbuf.tile([P, PASSES * NQ], U8, name=name + "_scales", align_bytes=64)
-            nc.vector.quantize_mx(
-                out=codes[:].bitcast(FP8X4), scales=scales[:], in_=rounded[:].rearrange("p o q j -> p (o q j)")
-            )
-            return codes, scales
+        def part_words(pairs, copies, name):
+            words = sbuf.tile([P, copies, PASSES, SLOTS // copies], U16, name=name + "_words", align_bytes=64)
+            halves = pairs[:].bitcast(U16).rearrange("p (c n o) -> p c o n", c=copies, o=PASSES)
+            for c in range(copies):
+                nc.vector.tensor_copy(words[:, c], halves[:, c])
+            width = SLOTS // copies
+            return [words[:, g // width, :, g % width : g % width + GROUP] for g in range(0, SLOTS, GROUP)]
 
         c_list = load_list(offs2, "c_list")
         k_list = load_list(offs, "k_list")
+        c_scale_window = load_scales(c_scales, "c_scale_window")
+        k_scale_window = load_scales(k_scales, "k_scale_window")
+        q_raw = sbuf.tile([P, PASSES, PACK, NQ], F32, name="q_raw")
+        nc.scalar.dma_start(q_raw[:], qT[0].rearrange("(o p j) q -> p o j q", o=PASSES, j=PACK))
+        c_word_window = load_words(c_words, nc.sync, "c_word_window")
+        k_word_window = load_words(k_words, nc.sync, "k_word_window")
         weight = sbuf.tile([P, 1], F32, name="weight")
         nc.sync.dma_start(weight[:], rw[0])
-        c_scale_window = load_scales(c_scales, nc.vector, "c_scale_window")
-        k_scale_window = load_scales(k_scales, nc.gpsimd, "k_scale_window")
-        c_word_window = load_words(c_words, nc.sync, "c_word_window")
-        q_raw = sbuf.tile([P, PASSES, PACK, NQ], F32, name="q_raw")
-        nc.sync.dma_start(q_raw[:], qT[0].rearrange("(o p j) q -> p o j q", o=PASSES, j=PACK))
-        k_word_window = load_words(k_words, nc.sync, "k_word_window")
 
         diffs = [psum.tile([NQ, GROUP], F32, name=f"diff{g}") for g in range(GROUPS)]
 
-        def multiply(g, query, words, planes, opens):
-            codes, scales = query
+        def multiply(g, sign, words, planes):
+            opens = sign == 0
             for o in range(PASSES):
-                cols = slice(o * NQ, (o + 1) * NQ)
+                cols = slice((sign * PASSES + o) * NQ, (sign * PASSES + o + 1) * NQ)
                 nc.tensor.matmul_mx(
                     out=diffs[g][:],
                     lhsT=codes[:, cols].bitcast(FP8X4),
@@ -104,22 +103,28 @@ def tile_attend_logrank_topk_kernel(tc, qT, k_words, k_scales, c_words, c_scales
                     stop=(not opens and o == PASSES - 1),
                 )
 
-        half = SLOTS // 2
         c_planes = gather_scales(c_scale_window, c_list, [nc.sync] * 4, "c_scale")
         k_planes = gather_scales(k_scale_window, k_list, [nc.sync] * 4, "k_scale")
-        c_listed = gather_words(c_word_window, c_list, 0, SLOTS, "c", "c_pairs")
-        q_plus = quantise(q_raw, 1.0, "q_plus")
-        q_minus = quantise(q_raw, -1.0, "q_minus")
+        c_pairs = gather_words(c_word_window, c_list, 1, "c", "c_pairs")
+
+        rounded = sbuf.tile([P, 2, PASSES, NQ, PACK], BF16, name="rounded", tag="rounded", align_bytes=64)
+        nc.scalar.activation(rounded[:, 0], q_raw[:].rearrange("p o j q -> p o q j"), ACT.Copy)
+        flat = rounded[:].rearrange("p s o q j -> p s (o q j)")
+        nc.scalar.activation(flat[:, 1], flat[:, 0], ACT.Copy, scale=-1.0)
+        codes = sbuf.tile([P, 2 * PASSES * NQ], U32, name="codes", align_bytes=64)
+        scales = sbuf.tile([P, 2 * PASSES * NQ], U8, name="scales", align_bytes=64)
+        nc.vector.quantize_mx(out=codes[:].bitcast(FP8X4), scales=scales[:], in_=flat.rearrange("p s n -> p (s n)"))
+
+        c_listed = part_words(c_pairs, 1, "c")
         for g in range(GROUPS):
-            multiply(g, q_plus, c_listed[g], c_planes, True)
-        k_listed = []
-        for h in range(2):
-            k_listed.extend(gather_words(k_word_window, k_list, h * half, half, f"k{h}", ["q_plus_bf16", "q_minus_bf16"][h]))
+            multiply(g, 0, c_listed[g], c_planes)
+        k_pairs = gather_words(k_word_window, k_list, 2, "k", "rounded")
+        k_listed = part_words(k_pairs, GROUPS, "k")
 
         grown = sbuf.tile([NQ, SLOTS], F32, name="grown")
         beyond = sbuf.tile([NQ, SLOTS], F32, name="beyond")
         for g in range(GROUPS):
-            multiply(g, q_minus, k_listed[g], k_planes, False)
+            multiply(g, 1, k_listed[g], k_planes)
             nc.scalar.activation(grown[:, g * GROUP : (g + 1) * GROUP], diffs[g][:], ACT.Exp)
         capped = sbuf.tile([NQ, SLOTS], F32, name="capped")
         nc.vector.tensor_scalar(capped[:], grown[:], math.exp(CAP), 1.0, ALU.min, ALU.add)

@@ -48,18 +48,6 @@ def tile_attend_logrank_topk_kernel(tc, qT, k_words, k_scales, c_words, c_scales
             queue.dma_start(t[:].bitcast(I32), src[0].rearrange("p t b -> p (t b)").bitcast(I32))
             return t
 
-        def gather_scales(window, idx, queues, name):
-            listed = sbuf.tile([P, SLOTS], U8, name=name + "_listed", align_bytes=64)
-            planes = sbuf.tile([P, PASSES, SLOTS], U8, name=name + "_planes", align_bytes=64)
-            nc.vector.memset(planes[:].rearrange("p o n -> p (o n)").bitcast(I32), 0)
-            nc.vector.tensor_copy(listed[:], window[:].indirect(idx[:]))
-            for quadrant in range(4):
-                first = 32 * quadrant
-                queues[quadrant].dma_start(
-                    planes[first : first + 4, :, :].bitcast(I32), listed[first : first + 32 : 4, :].bitcast(I32)
-                )
-            return planes
-
         def gather_words(window, idx, gathers, name, tag):
             pairs = sbuf.tile([P, SLOTS], U32, name=name + "_pairs", tag=tag, align_bytes=64)
             columns = SLOTS // 16 // gathers
@@ -77,19 +65,19 @@ def tile_attend_logrank_topk_kernel(tc, qT, k_words, k_scales, c_words, c_scales
             return [words[:, g // width, :, g % width : g % width + GROUP] for g in range(0, SLOTS, GROUP)]
 
         c_list = load_list(offs2, "c_list")
-        k_list = load_list(offs, "k_list")
         c_scale_window = load_scales(c_scales, "c_scale_window")
-        k_scale_window = load_scales(k_scales, "k_scale_window")
         q_raw = sbuf.tile([P, PASSES, PACK, NQ], F32, name="q_raw")
-        nc.scalar.dma_start(q_raw[:], qT[0].rearrange("(o p j) q -> p o j q", o=PASSES, j=PACK))
+        nc.sync.dma_start(q_raw[:], qT[0].rearrange("(o p j) q -> p o j q", o=PASSES, j=PACK))
+        k_list = load_list(offs, "k_list")
+        k_scale_window = load_scales(k_scales, "k_scale_window")
         c_word_window = load_words(c_words, nc.sync, "c_word_window")
-        k_word_window = load_words(k_words, nc.sync, "k_word_window")
         weight = sbuf.tile([P, 1], F32, name="weight")
         nc.sync.dma_start(weight[:], rw[0])
+        k_word_window = load_words(k_words, nc.sync, "k_word_window")
 
         diffs = [psum.tile([NQ, GROUP], F32, name=f"diff{g}") for g in range(GROUPS)]
 
-        def multiply(g, sign, words, planes):
+        def multiply(g, sign, words):
             opens = sign == 0
             for o in range(PASSES):
                 cols = slice((sign * PASSES + o) * NQ, (sign * PASSES + o + 1) * NQ)
@@ -98,13 +86,21 @@ def tile_attend_logrank_topk_kernel(tc, qT, k_words, k_scales, c_words, c_scales
                     lhsT=codes[:, cols].bitcast(FP8X4),
                     lhsT_scale=scales[:, cols],
                     rhs=words[:, o, :].bitcast(FP4X4),
-                    rhs_scale=planes[:, o, g * GROUP : (g + 1) * GROUP],
+                    rhs_scale=planes[:, o, sign, g * GROUP : (g + 1) * GROUP],
                     start=(opens and o == 0),
                     stop=(not opens and o == PASSES - 1),
                 )
 
-        c_planes = gather_scales(c_scale_window, c_list, [nc.sync] * 4, "c_scale")
-        k_planes = gather_scales(k_scale_window, k_list, [nc.sync] * 4, "k_scale")
+        listed = sbuf.tile([P, 2, SLOTS], U8, name="listed", align_bytes=64)
+        planes = sbuf.tile([P, PASSES, 2, SLOTS], U8, name="planes", align_bytes=64)
+        nc.vector.memset(planes[:].rearrange("p o s n -> p (o s n)").bitcast(I32), 0)
+        nc.vector.tensor_copy(listed[:, 0], c_scale_window[:].indirect(c_list[:]))
+        nc.vector.tensor_copy(listed[:, 1], k_scale_window[:].indirect(k_list[:]))
+        for first in range(0, P, 32):
+            nc.sync.dma_start(
+                planes[first : first + 4].rearrange("p o s n -> p (o s n)").bitcast(I32),
+                listed[first : first + 32 : 4].rearrange("p s n -> p (s n)").bitcast(I32),
+            )
         c_pairs = gather_words(c_word_window, c_list, 1, "c", "c_pairs")
 
         rounded = sbuf.tile([P, 2, PASSES, NQ, PACK], BF16, name="rounded", tag="rounded", align_bytes=64)
@@ -113,18 +109,19 @@ def tile_attend_logrank_topk_kernel(tc, qT, k_words, k_scales, c_words, c_scales
         nc.scalar.activation(flat[:, 1], flat[:, 0], ACT.Copy, scale=-1.0)
         codes = sbuf.tile([P, 2 * PASSES * NQ], U32, name="codes", align_bytes=64)
         scales = sbuf.tile([P, 2 * PASSES * NQ], U8, name="scales", align_bytes=64)
-        nc.vector.quantize_mx(out=codes[:].bitcast(FP8X4), scales=scales[:], in_=flat.rearrange("p s n -> p (s n)"))
-
+        both = PASSES * NQ
+        nc.vector.quantize_mx(out=codes[:, :both].bitcast(FP8X4), scales=scales[:, :both], in_=flat[:, 0])
         c_listed = part_words(c_pairs, 1, "c")
+        nc.vector.quantize_mx(out=codes[:, both:].bitcast(FP8X4), scales=scales[:, both:], in_=flat[:, 1])
         for g in range(GROUPS):
-            multiply(g, 0, c_listed[g], c_planes)
-        k_pairs = gather_words(k_word_window, k_list, 2, "k", "rounded")
+            multiply(g, 0, c_listed[g])
+        k_pairs = gather_words(k_word_window, k_list, 2, "k", "k_pairs")
         k_listed = part_words(k_pairs, GROUPS, "k")
 
         grown = sbuf.tile([NQ, SLOTS], F32, name="grown")
         beyond = sbuf.tile([NQ, SLOTS], F32, name="beyond")
         for g in range(GROUPS):
-            multiply(g, 1, k_listed[g], k_planes)
+            multiply(g, 1, k_listed[g])
             nc.scalar.activation(grown[:, g * GROUP : (g + 1) * GROUP], diffs[g][:], ACT.Exp)
         capped = sbuf.tile([NQ, SLOTS], F32, name="capped")
         nc.vector.tensor_scalar(capped[:], grown[:], math.exp(CAP), 1.0, ALU.min, ALU.add)

@@ -39,8 +39,8 @@ def tile_attend_logrank_topk_kernel(tc, qT, k_words, k_scales, c_words, c_scales
 
         def load_scales(src, name):
             t = sbuf.tile([P, src.shape[2]], U8, name=name, tag=name, align_bytes=64)
-            nc.vector.memset(t[:].bitcast(I32), 0)
-            nc.sync.dma_start(t[0:P:4, :].bitcast(I32), src.rearrange("o f t -> f o t").bitcast(I32))
+            nc.vector.memset(t[0:96, :].bitcast(I32), 0)
+            nc.scalar.dma_start(t[96:P, :].bitcast(I32), src.rearrange("o f t -> f o t").bitcast(I32))
             return t
 
         def load_words(src, queue, name):
@@ -66,14 +66,14 @@ def tile_attend_logrank_topk_kernel(tc, qT, k_words, k_scales, c_words, c_scales
 
         c_list = load_list(offs2, "c_list")
         c_scale_window = load_scales(c_scales, "c_scale_window")
-        q_raw = sbuf.tile([P, PASSES, PACK, NQ], F32, name="q_raw")
-        nc.sync.dma_start(q_raw[:], qT[0].rearrange("(o p j) q -> p o j q", o=PASSES, j=PACK))
         k_list = load_list(offs, "k_list")
         k_scale_window = load_scales(k_scales, "k_scale_window")
+        q_raw = sbuf.tile([P, PASSES, PACK, NQ], F32, name="q_raw")
+        nc.sync.dma_start(q_raw[:], qT[0].rearrange("(o p j) q -> p o j q", o=PASSES, j=PACK))
         c_word_window = load_words(c_words, nc.sync, "c_word_window")
+        k_word_window = load_words(k_words, nc.sync, "k_word_window")
         weight = sbuf.tile([P, 1], F32, name="weight")
         nc.sync.dma_start(weight[:], rw[0])
-        k_word_window = load_words(k_words, nc.sync, "k_word_window")
 
         diffs = [psum.tile([NQ, GROUP], F32, name=f"diff{g}") for g in range(GROUPS)]
 
@@ -99,7 +99,7 @@ def tile_attend_logrank_topk_kernel(tc, qT, k_words, k_scales, c_words, c_scales
         for first in range(0, P, 32):
             nc.sync.dma_start(
                 planes[first : first + 4].rearrange("p o s n -> p (o s n)").bitcast(I32),
-                listed[first : first + 32 : 4].rearrange("p s n -> p (s n)").bitcast(I32),
+                listed[96 + first // 4 : 96 + first // 4 + 8].rearrange("p s n -> p (s n)").bitcast(I32),
             )
         c_pairs = gather_words(c_word_window, c_list, 1, "c", "c_pairs")
 

@@ -68,12 +68,12 @@ def tile_attend_logrank_topk_kernel(tc, qT, k_words, k_scales, c_words, c_scales
         c_scale_window = load_scales(c_scales, "c_scale_window")
         k_list = load_list(offs, "k_list")
         k_scale_window = load_scales(k_scales, "k_scale_window")
+        weight = sbuf.tile([P, 1], F32, name="weight")
+        nc.scalar.dma_start(weight[:], rw[0])
         q_raw = sbuf.tile([P, PASSES, PACK, NQ], F32, name="q_raw")
         nc.sync.dma_start(q_raw[:], qT[0].rearrange("(o p j) q -> p o j q", o=PASSES, j=PACK))
         c_word_window = load_words(c_words, nc.sync, "c_word_window")
         k_word_window = load_words(k_words, nc.sync, "k_word_window")
-        weight = sbuf.tile([P, 1], F32, name="weight")
-        nc.sync.dma_start(weight[:], rw[0])
 
         diffs = [psum.tile([NQ, GROUP], F32, name=f"diff{g}") for g in range(GROUPS)]
 
@@ -96,7 +96,7 @@ def tile_attend_logrank_topk_kernel(tc, qT, k_words, k_scales, c_words, c_scales
         nc.vector.memset(planes[:].rearrange("p o s n -> p (o s n)").bitcast(I32), 0)
         nc.vector.tensor_copy(listed[:, 0], c_scale_window[:].indirect(c_list[:]))
         nc.vector.tensor_copy(listed[:, 1], k_scale_window[:].indirect(k_list[:]))
-        for first in range(0, P, 32):
+        for first in (0, 64, 32, 96):
             nc.sync.dma_start(
                 planes[first : first + 4].rearrange("p o s n -> p (o s n)").bitcast(I32),
                 listed[96 + first // 4 : 96 + first // 4 + 8].rearrange("p s n -> p (s n)").bitcast(I32),

@@ -68,8 +68,6 @@ def tile_attend_logrank_topk_kernel(tc, qT, k_words, k_scales, c_words, c_scales
         c_scale_window = load_scales(c_scales, "c_scale_window")
         k_list = load_list(offs, "k_list")
         k_scale_window = load_scales(k_scales, "k_scale_window")
-        weight = sbuf.tile([P, 1], F32, name="weight")
-        nc.scalar.dma_start(weight[:], rw[0])
         q_raw = sbuf.tile([P, PASSES, PACK, NQ], F32, name="q_raw")
         nc.sync.dma_start(q_raw[:], qT[0].rearrange("(o p j) q -> p o j q", o=PASSES, j=PACK))
         c_word_window = load_words(c_words, nc.sync, "c_word_window")
@@ -101,6 +99,8 @@ def tile_attend_logrank_topk_kernel(tc, qT, k_words, k_scales, c_words, c_scales
                 planes[first : first + 4].rearrange("p o s n -> p (o s n)").bitcast(I32),
                 listed[96 + first // 4 : 96 + first // 4 + 8].rearrange("p s n -> p (s n)").bitcast(I32),
             )
+        weight = sbuf.tile([P, 1], F32, name="weight")
+        nc.sync.dma_start(weight[:], rw[0])
         c_pairs = gather_words(c_word_window, c_list, 1, "c", "c_pairs")
 
         rounded = sbuf.tile([P, 2, PASSES, NQ, PACK], BF16, name="rounded", tag="rounded", align_bytes=64)

@@ -104,7 +104,12 @@ def tile_attend_logrank_topk_kernel(tc, qT, k_words, k_scales, c_words, c_scales
         c_pairs = gather_words(c_word_window, c_list, 1, "c", "c_pairs")
 
         rounded = sbuf.tile([P, 2, PASSES, NQ, PACK], BF16, name="rounded", tag="rounded", align_bytes=64)
-        nc.scalar.activation(rounded[:, 0], q_raw[:].rearrange("p o j q -> p o q j"), ACT.Copy)
+        for o in range(PASSES):
+            nc.scalar.activation(
+                rounded[:, 0, o].rearrange("p (c i) j -> p c j i", i=PACK),
+                q_raw[:, o].rearrange("p j (c i) -> p c j i", i=PACK),
+                ACT.Copy,
+            )
         flat = rounded[:].rearrange("p s o q j -> p s (o q j)")
         nc.scalar.activation(flat[:, 1], flat[:, 0], ACT.Copy, scale=-1.0)
         codes = sbuf.tile([P, 2 * PASSES * NQ], U32, name="codes", align_bytes=64)

@@ -18,7 +18,6 @@ NQ = 128
 SLOTS = 512
 PASSES = 2
 PACK = 4
-SHIFT = 16
 CAP = 40.0
 GROUP = 128
 GROUPS = SLOTS // GROUP
@@ -39,89 +38,91 @@ def tile_attend_logrank_topk_kernel(tc, qT, k_words, k_scales, c_words, c_scales
 
         def load_scales(src, name):
             t = sbuf.tile([P, src.shape[2]], U8, name=name, tag=name, align_bytes=64)
+            rows = src.rearrange("o f t -> f o t").bitcast(I32)
             nc.vector.memset(t[0:96, :].bitcast(I32), 0)
-            nc.scalar.dma_start(t[96:P, :].bitcast(I32), src.rearrange("o f t -> f o t").bitcast(I32))
+            nc.scalar.dma_start(t[96:P, :].bitcast(I32), rows)
             return t
 
-        def load_words(src, queue, name):
+        def load_words(src, name):
             t = sbuf.tile([P, src.shape[2]], U32, name=name, align_bytes=64)
-            queue.dma_start(t[:].bitcast(I32), src[0].rearrange("p t b -> p (t b)").bitcast(I32))
+            nc.scalar.dma_start(t[:].bitcast(I32), src[0].rearrange("p t b -> p (t b)").bitcast(I32))
             return t
 
-        def gather_words(window, idx, gathers, name, tag):
-            pairs = sbuf.tile([P, SLOTS], U32, name=name + "_pairs", tag=tag, align_bytes=64)
-            columns = SLOTS // 16 // gathers
-            for n in range(gathers):
-                part = idx[:, n * columns : (n + 1) * columns]
-                nc.vector.tensor_copy(pairs[:, 16 * n * columns : 16 * (n + 1) * columns], window[:].indirect(part))
-            return pairs
+        def gather_words(window, idx, first, count, name, tag):
+            pairs = sbuf.tile([P, count], U32, name=name, tag=tag, align_bytes=64)
+            nc.vector.tensor_copy(pairs[:], window[:].indirect(idx[:, first // 16 : (first + count) // 16]))
+            return pairs[:]
 
-        def part_words(pairs, copies, name):
-            words = sbuf.tile([P, copies, PASSES, SLOTS // copies], U16, name=name + "_words", align_bytes=64)
-            halves = pairs[:].bitcast(U16).rearrange("p (c n o) -> p c o n", c=copies, o=PASSES)
-            for c in range(copies):
-                nc.vector.tensor_copy(words[:, c], halves[:, c])
-            width = SLOTS // copies
-            return [words[:, g // width, :, g % width : g % width + GROUP] for g in range(0, SLOTS, GROUP)]
+        def part_words(pairs, name, tag):
+            count = pairs.shape[1]
+            words = sbuf.tile([P, PASSES, count], U16, name=name, tag=tag, align_bytes=64)
+            nc.vector.tensor_copy(words[:], pairs.bitcast(U16).rearrange("p (n o) -> p o n", o=PASSES))
+            return [words[:, :, g : g + GROUP] for g in range(0, count, GROUP)]
 
         c_list = load_list(offs2, "c_list")
         c_scale_window = load_scales(c_scales, "c_scale_window")
         k_list = load_list(offs, "k_list")
         k_scale_window = load_scales(k_scales, "k_scale_window")
         q_raw = sbuf.tile([P, PASSES, PACK, NQ], F32, name="q_raw")
-        nc.sync.dma_start(q_raw[:], qT[0].rearrange("(o p j) q -> p o j q", o=PASSES, j=PACK))
-        c_word_window = load_words(c_words, nc.sync, "c_word_window")
-        k_word_window = load_words(k_words, nc.sync, "k_word_window")
+        nc.scalar.dma_start(q_raw[:], qT[0].rearrange("(o p j) q -> p o j q", o=PASSES, j=PACK))
+        c_word_window = load_words(c_words, "c_word_window")
+        k_word_window = load_words(k_words, "k_word_window")
 
         diffs = [psum.tile([NQ, GROUP], F32, name=f"diff{g}") for g in range(GROUPS)]
 
         def multiply(g, sign, words):
             opens = sign == 0
             for o in range(PASSES):
-                cols = slice((sign * PASSES + o) * NQ, (sign * PASSES + o + 1) * NQ)
+                cols = slice(o * NQ, (o + 1) * NQ)
                 nc.tensor.matmul_mx(
                     out=diffs[g][:],
-                    lhsT=codes[:, cols].bitcast(FP8X4),
-                    lhsT_scale=scales[:, cols],
+                    lhsT=codes[sign][:, cols].bitcast(FP8X4),
+                    lhsT_scale=scales[sign][:, cols],
                     rhs=words[:, o, :].bitcast(FP4X4),
                     rhs_scale=planes[:, o, sign, g * GROUP : (g + 1) * GROUP],
                     start=(opens and o == 0),
                     stop=(not opens and o == PASSES - 1),
                 )
 
-        listed = sbuf.tile([P, 2, SLOTS], U8, name="listed", align_bytes=64)
+        listed = sbuf.tile([P, 2, SLOTS], U8, name="listed", tag="listed", align_bytes=64)
         planes = sbuf.tile([P, PASSES, 2, SLOTS], U8, name="planes", align_bytes=64)
         nc.vector.memset(planes[:].rearrange("p o s n -> p (o s n)").bitcast(I32), 0)
         nc.vector.tensor_copy(listed[:, 0], c_scale_window[:].indirect(c_list[:]))
         nc.vector.tensor_copy(listed[:, 1], k_scale_window[:].indirect(k_list[:]))
-        for first in (0, 64, 32, 96):
-            nc.sync.dma_start(
-                planes[first : first + 4].rearrange("p o s n -> p (o s n)").bitcast(I32),
-                listed[96 + first // 4 : 96 + first // 4 + 8].rearrange("p s n -> p (s n)").bitcast(I32),
-            )
-        weight = sbuf.tile([P, 1], F32, name="weight")
-        nc.sync.dma_start(weight[:], rw[0])
-        c_pairs = gather_words(c_word_window, c_list, 1, "c", "c_pairs")
 
-        rounded = sbuf.tile([P, 2, PASSES, NQ, PACK], BF16, name="rounded", tag="rounded", align_bytes=64)
+        both = PASSES * NQ
+        rounded = sbuf.tile([P, PASSES, NQ, PACK], BF16, name="rounded", tag="rounded", align_bytes=64)
         for o in range(PASSES):
             nc.scalar.activation(
-                rounded[:, 0, o].rearrange("p (c i) j -> p c j i", i=PACK),
+                rounded[:, o].rearrange("p (c i) j -> p c j i", i=PACK),
                 q_raw[:, o].rearrange("p j (c i) -> p c j i", i=PACK),
                 ACT.Copy,
             )
-        flat = rounded[:].rearrange("p s o q j -> p s (o q j)")
-        nc.scalar.activation(flat[:, 1], flat[:, 0], ACT.Copy, scale=-1.0)
-        codes = sbuf.tile([P, 2 * PASSES * NQ], U32, name="codes", align_bytes=64)
-        scales = sbuf.tile([P, 2 * PASSES * NQ], U8, name="scales", align_bytes=64)
-        both = PASSES * NQ
-        nc.vector.quantize_mx(out=codes[:, :both].bitcast(FP8X4), scales=scales[:, :both], in_=flat[:, 0])
-        c_listed = part_words(c_pairs, 1, "c")
-        nc.vector.quantize_mx(out=codes[:, both:].bitcast(FP8X4), scales=scales[:, both:], in_=flat[:, 1])
+        for first in (0, 64, 32, 96):
+            source = 96 + first // 4
+            nc.sync.dma_start(
+                planes[first : first + 4].rearrange("p o s n -> p (o s n)").bitcast(I32),
+                listed[source : source + 8].rearrange("p s n -> p (s n)").bitcast(I32),
+            )
+        weight = sbuf.tile([P, 1], F32, name="weight", tag="listed", align_bytes=64)
+        nc.sync.dma_start(weight[:], rw[0])
+        flat = rounded[:].rearrange("p o q j -> p (o q j)")
+        negated = sbuf.tile([P, both * PACK], BF16, name="negated", tag="negated", align_bytes=64)
+        nc.scalar.activation(negated[:], flat, ACT.Copy, scale=-1.0)
+        codes = [sbuf.tile([P, both], U32, name=f"codes{s}", align_bytes=64) for s in range(2)]
+        scales = [sbuf.tile([P, both], U8, name=f"scales{s}", align_bytes=64) for s in range(2)]
+        c_pairs = gather_words(c_word_window, c_list, 0, SLOTS, "c_pairs", "c_pairs")
+        nc.vector.quantize_mx(out=codes[0][:].bitcast(FP8X4), scales=scales[0][:], in_=flat)
+        nc.vector.quantize_mx(out=codes[1][:].bitcast(FP8X4), scales=scales[1][:], in_=negated[:])
+        c_listed = part_words(c_pairs, "c_words", "rounded")
         for g in range(GROUPS):
             multiply(g, 0, c_listed[g])
-        k_pairs = gather_words(k_word_window, k_list, 2, "k", "k_pairs")
-        k_listed = part_words(k_pairs, GROUPS, "k")
+        k_pairs = sbuf.tile([P, SLOTS], U32, name="k_pairs", tag="negated", align_bytes=64)
+        for h in range(2):
+            nc.vector.tensor_copy(k_pairs[:, 256 * h : 256 * (h + 1)], k_word_window[:].indirect(k_list[:, 16 * h : 16 * (h + 1)]))
+        k_listed = []
+        for g in range(GROUPS):
+            k_listed.extend(part_words(k_pairs[:, g * GROUP : (g + 1) * GROUP], f"k_words{g}", f"k_words{g}"))
 
         grown = sbuf.tile([NQ, SLOTS], F32, name="grown")
         beyond = sbuf.tile([NQ, SLOTS], F32, name="beyond")

@@ -63,7 +63,7 @@ def tile_attend_logrank_topk_kernel(tc, qT, k_words, k_scales, c_words, c_scales
         c_scale_window = load_scales(c_scales, "c_scale_window")
         k_list = load_list(offs, "k_list")
         k_scale_window = load_scales(k_scales, "k_scale_window")
-        q_raw = sbuf.tile([P, PASSES, PACK, NQ], F32, name="q_raw")
+        q_raw = sbuf.tile([P, PASSES, PACK, NQ], F32, name="q_raw", tag="q_raw", align_bytes=64)
         nc.scalar.dma_start(q_raw[:], qT[0].rearrange("(o p j) q -> p o j q", o=PASSES, j=PACK))
         c_word_window = load_words(c_words, "c_word_window")
         k_word_window = load_words(k_words, "k_word_window")
@@ -113,16 +113,19 @@ def tile_attend_logrank_topk_kernel(tc, qT, k_words, k_scales, c_words, c_scales
         scales = [sbuf.tile([P, both], U8, name=f"scales{s}", align_bytes=64) for s in range(2)]
         c_pairs = gather_words(c_word_window, c_list, 0, SLOTS, "c_pairs", "c_pairs")
         nc.vector.quantize_mx(out=codes[0][:].bitcast(FP8X4), scales=scales[0][:], in_=flat)
+        c_listed = part_words(c_pairs, "c_words", "q_raw")
         nc.vector.quantize_mx(out=codes[1][:].bitcast(FP8X4), scales=scales[1][:], in_=negated[:])
-        c_listed = part_words(c_pairs, "c_words", "rounded")
         for g in range(GROUPS):
             multiply(g, 0, c_listed[g])
-        k_pairs = sbuf.tile([P, SLOTS], U32, name="k_pairs", tag="negated", align_bytes=64)
-        for h in range(2):
-            nc.vector.tensor_copy(k_pairs[:, 256 * h : 256 * (h + 1)], k_word_window[:].indirect(k_list[:, 16 * h : 16 * (h + 1)]))
+        k_pairs = sbuf.tile([P, 2, GROUP], U32, name="k_pairs", tag="rounded", align_bytes=64)
         k_listed = []
-        for g in range(GROUPS):
-            k_listed.extend(part_words(k_pairs[:, g * GROUP : (g + 1) * GROUP], f"k_words{g}", f"k_words{g}"))
+        for pair in range(GROUPS // 2):
+            for n in range(2):
+                g = 2 * pair + n
+                nc.vector.tensor_copy(k_pairs[:, n], k_word_window[:].indirect(k_list[:, 8 * g : 8 * (g + 1)]))
+            for n in range(2):
+                g = 2 * pair + n
+                k_listed.extend(part_words(k_pairs[:, n], f"k_words{g}", f"k_words{g}"))
 
         grown = sbuf.tile([NQ, SLOTS], F32, name="grown")
         beyond = sbuf.tile([NQ, SLOTS], F32, name="beyond")

@@ -117,15 +117,13 @@ def tile_attend_logrank_topk_kernel(tc, qT, k_words, k_scales, c_words, c_scales
         nc.vector.quantize_mx(out=codes[1][:].bitcast(FP8X4), scales=scales[1][:], in_=negated[:])
         for g in range(GROUPS):
             multiply(g, 0, c_listed[g])
-        k_pairs = sbuf.tile([P, 2, GROUP], U32, name="k_pairs", tag="rounded", align_bytes=64)
+        k_pairs = sbuf.tile([P, 3, GROUP], U32, name="k_pairs", tag="rounded", align_bytes=64)
         k_listed = []
-        for pair in range(GROUPS // 2):
-            for n in range(2):
-                g = 2 * pair + n
-                nc.vector.tensor_copy(k_pairs[:, n], k_word_window[:].indirect(k_list[:, 8 * g : 8 * (g + 1)]))
-            for n in range(2):
-                g = 2 * pair + n
-                k_listed.extend(part_words(k_pairs[:, n], f"k_words{g}", f"k_words{g}"))
+        for g in range(GROUPS + 1):
+            if g < GROUPS:
+                nc.vector.tensor_copy(k_pairs[:, g % 3], k_word_window[:].indirect(k_list[:, 8 * g : 8 * (g + 1)]))
+            if g > 0:
+                k_listed.extend(part_words(k_pairs[:, (g - 1) % 3], f"k_words{g - 1}", f"k_words{g - 1}"))
 
         grown = sbuf.tile([NQ, SLOTS], F32, name="grown")
         beyond = sbuf.tile([NQ, SLOTS], F32, name="beyond")
@@ -138,10 +136,12 @@ def tile_attend_logrank_topk_kernel(tc, qT, k_words, k_scales, c_words, c_scales
             nc.vector.tensor_scalar(beyond[:, g * GROUP : (g + 1) * GROUP], diffs[g][:], CAP, -CAP, ALU.max, ALU.add)
         beyond_w = sbuf.tile([NQ, SLOTS], F32, name="beyond_w")
         nc.vector.tensor_scalar(beyond_w[:], beyond[:], weight[:], None, ALU.mult)
-        for g in range(GROUPS):
-            cols = slice(g * GROUP, (g + 1) * GROUP)
-            logs = sbuf.tile([NQ, GROUP], F32, name=f"logs{g}")
+        first = 0
+        for n, (width, queue) in enumerate(zip((128, 128, 128, 128), (nc.sync, nc.sync, nc.sync, nc.sync))):
+            cols = slice(first, first + width)
+            first = first + width
+            logs = sbuf.tile([NQ, width], F32, name=f"logs{n}")
             nc.scalar.activation(logs[:], capped[:, cols], ACT.Ln)
-            result = sbuf.tile([NQ, GROUP], F32, name=f"result{g}")
+            result = sbuf.tile([NQ, width], F32, name=f"result{n}")
             nc.vector.scalar_tensor_tensor(result[:], logs[:], weight[:], beyond_w[:, cols], ALU.mult, ALU.add)
-            nc.sync.dma_start(out[0][:, cols], result[:])
+            queue.dma_start(out[0][:, cols], result[:])

@@ -118,12 +118,19 @@ def tile_attend_logrank_topk_kernel(tc, qT, k_words, k_scales, c_words, c_scales
         for g in range(GROUPS):
             multiply(g, 0, c_listed[g])
         k_pairs = sbuf.tile([P, 3, GROUP], U32, name="k_pairs", tag="rounded", align_bytes=64)
-        k_listed = []
-        for g in range(GROUPS + 1):
-            if g < GROUPS:
-                nc.vector.tensor_copy(k_pairs[:, g % 3], k_word_window[:].indirect(k_list[:, 8 * g : 8 * (g + 1)]))
-            if g > 0:
-                k_listed.extend(part_words(k_pairs[:, (g - 1) % 3], f"k_words{g - 1}", f"k_words{g - 1}"))
+
+        def gather_keys(g, count):
+            into = k_pairs[:, g % 3 : g % 3 + count].rearrange("p g n -> p (g n)")
+            nc.vector.tensor_copy(into, k_word_window[:].indirect(k_list[:, 8 * g : 8 * (g + count)]))
+
+        def part_keys(g):
+            return part_words(k_pairs[:, g % 3], f"k_words{g}", f"k_words{g}")[0]
+
+        gather_keys(0, 2)
+        gather_keys(2, 1)
+        k_listed = [part_keys(0), part_keys(1)]
+        gather_keys(3, 1)
+        k_listed.extend([part_keys(2), part_keys(3)])
 
         grown = sbuf.tile([NQ, SLOTS], F32, name="grown")
         beyond = sbuf.tile([NQ, SLOTS], F32, name="beyond")

@@ -36,11 +36,11 @@ def tile_attend_logrank_topk_kernel(tc, qT, k_words, k_scales, c_words, c_scales
             nc.sync.dma_start(t[:], src)
             return t
 
-        def load_scales(src, name):
+        def load_scales(src, name, queue):
             t = sbuf.tile([P, src.shape[2]], U8, name=name, tag=name, align_bytes=64)
             rows = src.rearrange("o f t -> f o t").bitcast(I32)
             nc.vector.memset(t[0:96, :].bitcast(I32), 0)
-            nc.scalar.dma_start(t[96:P, :].bitcast(I32), rows)
+            queue.dma_start(t[96:P, :].bitcast(I32), rows)
             return t
 
         def load_words(src, name):
@@ -60,9 +60,9 @@ def tile_attend_logrank_topk_kernel(tc, qT, k_words, k_scales, c_words, c_scales
             return [words[:, :, g : g + GROUP] for g in range(0, count, GROUP)]
 
         c_list = load_list(offs2, "c_list")
-        c_scale_window = load_scales(c_scales, "c_scale_window")
+        c_scale_window = load_scales(c_scales, "c_scale_window", nc.scalar)
+        k_scale_window = load_scales(k_scales, "k_scale_window", nc.sync)
         k_list = load_list(offs, "k_list")
-        k_scale_window = load_scales(k_scales, "k_scale_window")
         q_raw = sbuf.tile([P, PASSES, PACK, NQ], F32, name="q_raw", tag="q_raw", align_bytes=64)
         nc.scalar.dma_start(q_raw[:], qT[0].rearrange("(o p j) q -> p o j q", o=PASSES, j=PACK))
         c_word_window = load_words(c_words, "c_word_window")

@@ -143,12 +143,11 @@ def tile_attend_logrank_topk_kernel(tc, qT, k_words, k_scales, c_words, c_scales
             nc.vector.tensor_scalar(beyond[:, g * GROUP : (g + 1) * GROUP], diffs[g][:], CAP, -CAP, ALU.max, ALU.add)
         beyond_w = sbuf.tile([NQ, SLOTS], F32, name="beyond_w")
         nc.vector.tensor_scalar(beyond_w[:], beyond[:], weight[:], None, ALU.mult)
-        first = 0
-        for n, (width, queue) in enumerate(zip((128, 128, 128, 128), (nc.sync, nc.sync, nc.sync, nc.sync))):
-            cols = slice(first, first + width)
-            first = first + width
-            logs = sbuf.tile([NQ, width], F32, name=f"logs{n}")
-            nc.scalar.activation(logs[:], capped[:, cols], ACT.Ln)
-            result = sbuf.tile([NQ, width], F32, name=f"result{n}")
-            nc.vector.scalar_tensor_tensor(result[:], logs[:], weight[:], beyond_w[:, cols], ALU.mult, ALU.add)
-            queue.dma_start(out[0][:, cols], result[:])
+        logs = sbuf.tile([NQ, SLOTS], F32, name="logs")
+        result = sbuf.tile([NQ, SLOTS], F32, name="result")
+        pieces = [slice(g * GROUP, (g + 1) * GROUP) for g in range(GROUPS)]
+        for cols in pieces:
+            nc.scalar.activation(logs[:, cols], capped[:, cols], ACT.Ln)
+        for cols, queue in zip(pieces, (nc.sync, nc.scalar, nc.sync, nc.scalar)):
+            nc.vector.scalar_tensor_tensor(result[:, cols], logs[:, cols], weight[:], beyond_w[:, cols], ALU.mult, ALU.add)
+            queue.dma_start(out[0][:, cols], result[:, cols])

@@ -57,7 +57,7 @@ def tile_attend_logrank_topk_kernel(tc, qT, k_words, k_scales, c_words, c_scales
             count = pairs.shape[1]
             words = sbuf.tile([P, PASSES, count], U16, name=name, tag=tag, align_bytes=64)
             nc.vector.tensor_copy(words[:], pairs.bitcast(U16).rearrange("p (n o) -> p o n", o=PASSES))
-            return [words[:, :, g : g + GROUP] for g in range(0, count, GROUP)]
+            return words
 
         c_list = load_list(offs2, "c_list")
         c_scale_window = load_scales(c_scales, "c_scale_window", nc.scalar)
@@ -68,20 +68,20 @@ def tile_attend_logrank_topk_kernel(tc, qT, k_words, k_scales, c_words, c_scales
         c_word_window = load_words(c_words, "c_word_window")
         k_word_window = load_words(k_words, "k_word_window")
 
-        diffs = [psum.tile([NQ, GROUP], F32, name=f"diff{g}") for g in range(GROUPS)]
+        spans = [slice(0, 2 * GROUP), slice(2 * GROUP, 3 * GROUP), slice(3 * GROUP, SLOTS)]
+        diffs = [psum.tile([NQ, span.stop - span.start], F32, name=f"diff{g}") for g, span in enumerate(spans)]
 
-        def multiply(g, sign, words):
-            opens = sign == 0
+        def multiply(bank, sign, words, slots, opens, closes):
             for o in range(PASSES):
                 cols = slice(o * NQ, (o + 1) * NQ)
                 nc.tensor.matmul_mx(
-                    out=diffs[g][:],
+                    out=bank,
                     lhsT=codes[sign][:, cols].bitcast(FP8X4),
                     lhsT_scale=scales[sign][:, cols],
                     rhs=words[:, o, :].bitcast(FP4X4),
-                    rhs_scale=planes[:, o, sign, g * GROUP : (g + 1) * GROUP],
+                    rhs_scale=planes[:, o, sign, slots],
                     start=(opens and o == 0),
-                    stop=(not opens and o == PASSES - 1),
+                    stop=(closes and o == PASSES - 1),
                 )
 
         listed = sbuf.tile([P, 2, SLOTS], U8, name="listed", tag="listed", align_bytes=64)
@@ -115,32 +115,35 @@ def tile_attend_logrank_topk_kernel(tc, qT, k_words, k_scales, c_words, c_scales
         nc.vector.quantize_mx(out=codes[0][:].bitcast(FP8X4), scales=scales[0][:], in_=flat)
         c_listed = part_words(c_pairs, "c_words", "q_raw")
         nc.vector.quantize_mx(out=codes[1][:].bitcast(FP8X4), scales=scales[1][:], in_=negated[:])
-        for g in range(GROUPS):
-            multiply(g, 0, c_listed[g])
+        for g, span in enumerate(spans):
+            multiply(diffs[g][:], 0, c_listed[:, :, span], span, True, False)
         k_pairs = sbuf.tile([P, 3, GROUP], U32, name="k_pairs", tag="rounded", align_bytes=64)
 
         def gather_keys(g, count):
             into = k_pairs[:, g % 3 : g % 3 + count].rearrange("p g n -> p (g n)")
             nc.vector.tensor_copy(into, k_word_window[:].indirect(k_list[:, 8 * g : 8 * (g + count)]))
 
-        def part_keys(g):
-            return part_words(k_pairs[:, g % 3], f"k_words{g}", f"k_words{g}")[0]
+        def part_keys(g, count):
+            pairs = k_pairs[:, g % 3 : g % 3 + count].rearrange("p g n -> p (g n)")
+            return part_words(pairs, f"k_words{g}", f"k_words{g}")
 
         gather_keys(0, 2)
         gather_keys(2, 1)
-        k_listed = [part_keys(0), part_keys(1)]
+        k_listed = [part_keys(0, 1), part_keys(1, 1)]
         gather_keys(3, 1)
-        k_listed.extend([part_keys(2), part_keys(3)])
+        k_listed.extend([part_keys(2, 1), part_keys(3, 1)])
 
         grown = sbuf.tile([NQ, SLOTS], F32, name="grown")
         beyond = sbuf.tile([NQ, SLOTS], F32, name="beyond")
-        for g in range(GROUPS):
-            multiply(g, 1, k_listed[g])
-            nc.scalar.activation(grown[:, g * GROUP : (g + 1) * GROUP], diffs[g][:], ACT.Exp)
+        for g, span in enumerate(spans):
+            for first in range(span.start, span.stop, GROUP):
+                into = diffs[g][:, first - span.start : first - span.start + GROUP]
+                multiply(into, 1, k_listed[first // GROUP], slice(first, first + GROUP), False, first + GROUP == span.stop)
+            nc.scalar.activation(grown[:, span], diffs[g][:], ACT.Exp)
         capped = sbuf.tile([NQ, SLOTS], F32, name="capped")
         nc.vector.tensor_scalar(capped[:], grown[:], math.exp(CAP), 1.0, ALU.min, ALU.add)
-        for g in range(GROUPS):
-            nc.vector.tensor_scalar(beyond[:, g * GROUP : (g + 1) * GROUP], diffs[g][:], CAP, -CAP, ALU.max, ALU.add)
+        for g, span in enumerate(spans):
+            nc.vector.tensor_scalar(beyond[:, span], diffs[g][:], CAP, -CAP, ALU.max, ALU.add)
         beyond_w = sbuf.tile([NQ, SLOTS], F32, name="beyond_w")
         nc.vector.tensor_scalar(beyond_w[:], beyond[:], weight[:], None, ALU.mult)
         logs = sbuf.tile([NQ, SLOTS], F32, name="logs")

@@ -61,7 +61,7 @@ def tile_attend_logrank_topk_kernel(tc, qT, k_words, k_scales, c_words, c_scales
 
         c_list = load_list(offs2, "c_list")
         c_scale_window = load_scales(c_scales, "c_scale_window", nc.scalar)
-        k_scale_window = load_scales(k_scales, "k_scale_window", nc.sync)
+        k_scale_window = load_scales(k_scales, "k_scale_window", nc.scalar)
         k_list = load_list(offs, "k_list")
         q_raw = sbuf.tile([P, PASSES, PACK, NQ], F32, name="q_raw", tag="q_raw", align_bytes=64)
         nc.scalar.dma_start(q_raw[:], qT[0].rearrange("(o p j) q -> p o j q", o=PASSES, j=PACK))
@@ -151,6 +151,6 @@ def tile_attend_logrank_topk_kernel(tc, qT, k_words, k_scales, c_words, c_scales
         pieces = [slice(g * GROUP, (g + 1) * GROUP) for g in range(GROUPS)]
         for cols in pieces:
             nc.scalar.activation(logs[:, cols], capped[:, cols], ACT.Ln)
-        for cols, queue in zip(pieces, (nc.sync, nc.scalar, nc.sync, nc.scalar)):
+        for cols, queue in zip(pieces, (nc.sync, nc.scalar, nc.sync, nc.sync)):
             nc.vector.scalar_tensor_tensor(result[:, cols], logs[:, cols], weight[:], beyond_w[:, cols], ALU.mult, ALU.add)
             queue.dma_start(out[0][:, cols], result[:, cols])

import math

import concourse.mybir as mybir

F32 = mybir.dt.float32
BF16 = mybir.dt.bfloat16
I32 = mybir.dt.int32
U32 = mybir.dt.uint32
U16 = mybir.dt.uint16
U8 = mybir.dt.uint8
FP8X4 = mybir.dt.float8_e4m3fn_x4
FP4X4 = mybir.dt.float4_e2m1fn_x4
ACT = mybir.ActivationFunctionType
ALU = mybir.AluOpType

P = 128
NQ = 128
SLOTS = 512
PASSES = 2
PACK = 4
CAP = 40.0
GROUP = 128
GROUPS = SLOTS // GROUP

FLOPS = 2 * 2 * NQ * SLOTS * 1024


def tile_attend_logrank_topk_kernel(tc, qT, k_words, k_scales, c_words, c_scales, rw, offs, offs2, out):
    nc = tc.nc
    with (
        tc.tile_pool(name="sbuf", bufs=1) as sbuf,
        tc.psum_pool(name="psum", bufs=1) as psum,
    ):
        def load_list(src, name):
            t = sbuf.tile([P, SLOTS // 16], U16, name=name)
            nc.sync.dma_start(t[:], src)
            return t

        def load_scales(src, name, queue):
            t = sbuf.tile([P, src.shape[2]], U8, name=name, tag=name, align_bytes=64)
            rows = src.rearrange("o f t -> f o t").bitcast(I32)
            nc.vector.memset(t[0:96, :].bitcast(I32), 0)
            queue.dma_start(t[96:P, :].bitcast(I32), rows)
            return t

        def load_words(src, name):
            t = sbuf.tile([P, src.shape[2]], U32, name=name, align_bytes=64)
            nc.scalar.dma_start(t[:].bitcast(I32), src[0].rearrange("p t b -> p (t b)").bitcast(I32))
            return t

        def gather_words(window, idx, first, count, name, tag):
            pairs = sbuf.tile([P, count], U32, name=name, tag=tag, align_bytes=64)
            nc.vector.tensor_copy(pairs[:], window[:].indirect(idx[:, first // 16 : (first + count) // 16]))
            return pairs[:]

        def part_words(pairs, name, tag):
            count = pairs.shape[1]
            words = sbuf.tile([P, PASSES, count], U16, name=name, tag=tag, align_bytes=64)
            nc.vector.tensor_copy(words[:], pairs.bitcast(U16).rearrange("p (n o) -> p o n", o=PASSES))
            return words

        c_list = load_list(offs2, "c_list")
        c_scale_window = load_scales(c_scales, "c_scale_window", nc.scalar)
        k_scale_window = load_scales(k_scales, "k_scale_window", nc.scalar)
        k_list = load_list(offs, "k_list")
        q_raw = sbuf.tile([P, PASSES, PACK, NQ], F32, name="q_raw", tag="q_raw", align_bytes=64)
        nc.scalar.dma_start(q_raw[:], qT[0].rearrange("(o p j) q -> p o j q", o=PASSES, j=PACK))
        c_word_window = load_words(c_words, "c_word_window")
        k_word_window = load_words(k_words, "k_word_window")

        spans = [slice(0, 2 * GROUP), slice(2 * GROUP, 3 * GROUP), slice(3 * GROUP, SLOTS)]
        diffs = [psum.tile([NQ, span.stop - span.start], F32, name=f"diff{g}") for g, span in enumerate(spans)]

        def multiply(bank, sign, words, slots, opens, closes):
            for o in range(PASSES):
                cols = slice(o * NQ, (o + 1) * NQ)
                nc.tensor.matmul_mx(
                    out=bank,
                    lhsT=codes[sign][:, cols].bitcast(FP8X4),
                    lhsT_scale=scales[sign][:, cols],
                    rhs=words[:, o, :].bitcast(FP4X4),
                    rhs_scale=planes[:, o, sign, slots],
                    start=(opens and o == 0),
                    stop=(closes and o == PASSES - 1),
                )

        listed = sbuf.tile([P, 2, SLOTS], U8, name="listed", tag="listed", align_bytes=64)
        planes = sbuf.tile([P, PASSES, 2, SLOTS], U8, name="planes", align_bytes=64)
        nc.vector.memset(planes[:].rearrange("p o s n -> p (o s n)").bitcast(I32), 0)
        nc.vector.tensor_copy(listed[:, 0], c_scale_window[:].indirect(c_list[:]))
        nc.vector.tensor_copy(listed[:, 1], k_scale_window[:].indirect(k_list[:]))

        both = PASSES * NQ
        rounded = sbuf.tile([P, PASSES, NQ, PACK], BF16, name="rounded", tag="rounded", align_bytes=64)
        for o in range(PASSES):
            nc.scalar.activation(
                rounded[:, o].rearrange("p (c i) j -> p c j i", i=PACK),
                q_raw[:, o].rearrange("p j (c i) -> p c j i", i=PACK),
                ACT.Copy,
            )
        for first in (0, 64, 32, 96):
            source = 96 + first // 4
            nc.sync.dma_start(
                planes[first : first + 4].rearrange("p o s n -> p (o s n)").bitcast(I32),
                listed[source : source + 8].rearrange("p s n -> p (s n)").bitcast(I32),
            )
        weight = sbuf.tile([P, 1], F32, name="weight", tag="listed", align_bytes=64)
        nc.sync.dma_start(weight[:], rw[0])
        flat = rounded[:].rearrange("p o q j -> p (o q j)")
        negated = sbuf.tile([P, both * PACK], BF16, name="negated", tag="negated", align_bytes=64)
        nc.scalar.activation(negated[:], flat, ACT.Copy, scale=-1.0)
        codes = [sbuf.tile([P, both], U32, name=f"codes{s}", align_bytes=64) for s in range(2)]
        scales = [sbuf.tile([P, both], U8, name=f"scales{s}", align_bytes=64) for s in range(2)]
        c_pairs = gather_words(c_word_window, c_list, 0, SLOTS, "c_pairs", "c_pairs")
        nc.vector.quantize_mx(out=codes[0][:].bitcast(FP8X4), scales=scales[0][:], in_=flat)
        c_listed = part_words(c_pairs, "c_words", "q_raw")
        nc.vector.quantize_mx(out=codes[1][:].bitcast(FP8X4), scales=scales[1][:], in_=negated[:])
        for g, span in enumerate(spans):
            multiply(diffs[g][:], 0, c_listed[:, :, span], span, True, False)
        k_pairs = sbuf.tile([P, 3, GROUP], U32, name="k_pairs", tag="rounded", align_bytes=64)

        def gather_keys(g, count):
            into = k_pairs[:, g % 3 : g % 3 + count].rearrange("p g n -> p (g n)")
            nc.vector.tensor_copy(into, k_word_window[:].indirect(k_list[:, 8 * g : 8 * (g + count)]))

        def part_keys(g, count):
            pairs = k_pairs[:, g % 3 : g % 3 + count].rearrange("p g n -> p (g n)")
            return part_words(pairs, f"k_words{g}", f"k_words{g}")

        gather_keys(0, 2)
        gather_keys(2, 1)
        k_listed = [part_keys(0, 1), part_keys(1, 1)]
        gather_keys(3, 1)
        k_listed.extend([part_keys(2, 1), part_keys(3, 1)])

        grown = sbuf.tile([NQ, SLOTS], F32, name="grown")
        beyond = sbuf.tile([NQ, SLOTS], F32, name="beyond")
        for g, span in enumerate(spans):
            for first in range(span.start, span.stop, GROUP):
                into = diffs[g][:, first - span.start : first - span.start + GROUP]
                multiply(into, 1, k_listed[first // GROUP], slice(first, first + GROUP), False, first + GROUP == span.stop)
            nc.scalar.activation(grown[:, span], diffs[g][:], ACT.Exp)
        capped = sbuf.tile([NQ, SLOTS], F32, name="capped")
        nc.vector.tensor_scalar(capped[:], grown[:], math.exp(CAP), 1.0, ALU.min, ALU.add)
        for g, span in enumerate(spans):
            nc.vector.tensor_scalar(beyond[:, span], diffs[g][:], CAP, -CAP, ALU.max, ALU.add)
        beyond_w = sbuf.tile([NQ, SLOTS], F32, name="beyond_w")
        nc.vector.tensor_scalar(beyond_w[:], beyond[:], weight[:], None, ALU.mult)
        logs = sbuf.tile([NQ, SLOTS], F32, name="logs")
        result = sbuf.tile([NQ, SLOTS], F32, name="result")
        pieces = [slice(g * GROUP, (g + 1) * GROUP) for g in range(GROUPS)]
        for cols in pieces:
            nc.scalar.activation(logs[:, cols], capped[:, cols], ACT.Ln)
        for cols, queue in zip(pieces, (nc.sync, nc.scalar, nc.sync, nc.sync)):
            nc.vector.scalar_tensor_tensor(result[:, cols], logs[:, cols], weight[:], beyond_w[:, cols], ALU.mult, ALU.add)
            queue.dma_start(out[0][:, cols], result[:, cols])
